import numpy as np, ml_dtypes
CORES = [113,118,241,246]
N = 4
BF = ml_dtypes.bfloat16
def gentries(a):
    return np.ascontiguousarray(a.reshape(8, 16, -1).transpose(0, 2, 1)).reshape(8, -1)
def gtable(e):
    e = np.asarray(e); return np.ascontiguousarray(e.reshape(8, -1, 16).transpose(0, 2, 1)).reshape(128, -1).astype(np.int32)
M, Q, V, TOP = 2048, 256, 4, 15
WT = 15
def far_maps(rng):
    p = np.argsort(rng.random((N, 8, M)), axis=-1)
    return np.where(rng.random(p.shape) < 0.125, rng.integers(0, M, p.shape), p).astype(np.int32)
def lists(a):
    return np.stack([gtable(u) for u in a])
def setup_inputs(rng):
    return {"nx": far_maps(rng), "w": rng.integers(0, WT + 1, (N, 8, M)).astype(np.int32), "x": lists(rng.integers(0, M, (N, 8, Q))), "e": lists(rng.integers(0, TOP + 1, (N, 8, V * Q)))}
def setup_inputs_ends(rng):
    d = setup_inputs(rng); k = rng.choice(np.array([0, TOP]), (N, 8, V, Q))
    k[:, :, :, 0] = 0; k[:, :, :, 1] = TOP; k[:, :, :, Q - 1] = 0; k[:, :, V - 1, Q - 1] = TOP
    d["e"] = lists(k.reshape(N, 8, V * Q))
    w = np.where(rng.random((N, 8, M)) < 0.5, WT, 0); w[:, 0] = WT; d["w"] = w.astype(np.int32)
    return d
def setup_inputs_still(rng):
    d = setup_inputs(rng); a = np.array(d["nx"]); s = int(rng.integers(0, 4)); p = np.arange(M)
    for r in range(N):
        h = (r + s) % 4; c = rng.choice(np.arange(2, M - 1), 8, replace=False)
        if h == 0:
            a[r] = p
        elif h == 1:
            c[0] = 0; c[1] = M - 1; a[r] = rng.permutation(c)[:, None]
        elif h == 2:
            c[0] = 1; c[1] = M - 1; a[r] = (p + rng.permutation(c)[:, None]) % M
        else:
            c[0] = 1; c[1] = M - 1; a[r] = p ^ rng.permutation(c)[:, None]
    d["nx"] = a; return d
def setup_inputs_alike(rng):
    d = setup_inputs(rng); k = rng.integers(0, TOP + 1, (N, 8, V, Q // 2))
    z = np.where((np.arange(N)[:, None] + np.arange(8)) % 2 == 0, M - 1, 0)
    d["x"] = lists(np.repeat(z[:, :, None], Q, axis=2)); d["e"] = lists(np.concatenate([k, k], -1).reshape(N, 8, V * Q)); return d
def setup_inputs_spread(rng):
    d = setup_inputs(rng)
    d["nx"] = np.floor(M * rng.random((N, 8, M)) ** 3).astype(np.int32)
    d["w"] = np.floor((WT + 1) * rng.random((N, 8, M)) ** 4).astype(np.int32)
    d["x"] = lists(np.floor(M * rng.random((N, 8, Q)) ** 2)); d["e"] = lists(np.floor((TOP + 1) * rng.random((N, 8, V * Q)) ** 3)); return d
def check_inputs(d):
    bad = []
    for name, top in (("nx", M - 1), ("w", WT), ("x", M - 1), ("e", TOP)):
        if np.min(d[name]) < 0 or np.max(d[name]) > top: bad.append("range of " + name)
    return bad
def reference(nx, w, x, e):
    last = np.zeros((N, 128, Q // 16), np.int32); total = np.zeros((N, 128, Q // 16), np.int32); g = np.arange(8)[:, None]
    for r in range(N):
        p = gentries(x[r]).astype(np.int64); k = gentries(e[r]).reshape(8, V, Q); s = np.zeros((8, Q), np.int64)
        for t in range(V):
            q = (r + t) % N
            for i in range(TOP):
                go = i < k[:, t]
                s = s + np.where(go, w[q][g, p], 0)
                p = np.where(go, nx[q][g, p], p)
        last[r] = gtable(p); total[r] = gtable(s)
    return {"last": np.asarray(last, np.float32), "total": np.asarray(total, np.float32)}

@@ -1,0 +1,400 @@
+from concourse.mybir import AluOpType as A, ActivationFunctionType as AF
+
+NV = 4
+BIG = 16777216.0
+FAR = 32768.0
+CUT = 1088
+ZC = 1280
+
+SCRATCH = {"ps%d" % b: ("psum", [128, 512], "float32") for b in range(8)}
+for _n in ("sh1", "sh2", "sh4", "idn", "rep", "repf", "zz", "one", "s1", "sums", "w1", "sumw", "f512", "sumf"):
+    SCRATCH[_n] = ("sbuf", [128, 8, 16], "float16")
+SCRATCH["m16"] = ("sbuf", [128, 2, 8], "float16")
+SCRATCH["lrb"] = ("sbuf", [128, 4, 8, 16], "float16")
+for _dt, _bufs in (
+        ("int32", "base 512 lst 128 w0 2048 xi 16 ei 64 fo 16 fin 16 fp 16 ft 16"),
+        ("float16", "b16 512 g1 2048 g2 2048 g3 2048 lf1 128 lf2 128 mm0 256 mm1 256 mm2 256 mm3 256 mw0 256"
+                    " hx0 256 hx1 256 hx2 256 nfar 256 far 256 rr 144 y4 144"),
+        ("uint16", "l1 128 l2 128 l4 128 l8 128 eu 64 le1 32 le2 32 le3 16 off0 16 ho0 16 ho1 16 ho2 16"
+                   " land1 16 land2 16 land3 16"),
+        ("float32", "mt 16 ht 16 hi0 16 xo 16 sd 256 ta 2048 tb 2048 win 4096"
+                    " mk0 256 mk1 256 mk2 256 mk3 256 sc 256 sw 256 gw 256"
+                    " wl0 16 wl1 16 wl2 16 wr1 16 wr2 16 acc1 16 acc 16 ol 16 ot 16")):
+    _w = _bufs.split()
+    for _i in range(0, len(_w), 2):
+        SCRATCH[_w[_i]] = ("sbuf", [128, int(_w[_i + 1])], _dt)
+SEMAPHORES = ["v", "s", "pe", "gi", "lda", "ldl", "lde", "lw", "lx1", "lx2", "cp", "outs", "loc",
+              "ad1", "ad2", "ad3", "hop10", "hop11", "hop20", "hop21", "hop30", "hop31", "hop4", "bg1", "bg2"]
+
+
+def rank_program(g, core, T, topo):
+    rank = T.rank_of(core)
+    if rank is None:
+        return
+    V, S, PE, Y = g.vector, g.scalar, g.tensor, g.sync
+    sem = T.sem
+    peer = lambda d: T.cores[(rank + d) % NV]
+    cnt = {"v": 0, "s": 0, "pe": 0, "gi": 0, "loc": 0}
+
+    def done(name, ins):
+        ins.then_inc(sem[name], 1)
+        cnt[name] += 1
+        return cnt[name]
+
+    def vw(n):
+        V.wait_ge(sem.v, n)
+
+    def ts(out, in0, op, c, op1=None, c1=None):
+        if op1 is None:
+            return done("v", V.tensor_scalar(out=out, in0=in0, scalar1=c, scalar2=None, op0=op))
+        return done("v", V.tensor_scalar(out=out, in0=in0, scalar1=c, scalar2=c1, op0=op, op1=op1))
+
+    def tt(out, in0, in1, op=A.add):
+        return done("v", V.tensor_tensor(out=out, in0=in0, in1=in1, op=op))
+
+    def vcopy(out, in_):
+        return done("v", V.tensor_copy(out=out, in_=in_))
+
+    def fill(ap, c):
+        return done("v", V.memset(ap, c))
+
+    def act(out, in_, func=AF.Copy, bias=0.0, scale=1.0):
+        return done("s", S.activation(out=out, in_=in_, func=func, bias=bias, scale=scale))
+
+    def mm(out, lhsT, rhs, start, stop, count=True):
+        ins = PE.matmul(out=out, lhsT=lhsT, rhs=rhs, start=start, stop=stop)
+        return done("pe", ins) if count else 0
+
+    def iota(ap, pattern, cm=0, base=0):
+        return done("gi", g.iota(ap, pattern, base, cm, allow_small_or_imprecise_dtypes=True))
+
+    def sel(out, in_, pattern, op, c, base, cm):
+        return done("gi", g.affine_select(out, in_, pattern, op, c, base, cm))
+
+    ps = [T["ps%d" % b] for b in range(8)]
+    cols = lambda t, q: t[:, 512 * q:512 * q + 512]
+    al = lambda name: T[name][:, :, :]
+
+    Y.dma_start(out=T.lst[:, :], in_=T.nx[:]).then_inc(sem.ldl, 16)
+    S.dma_start(out=T.base[32:64, :], in_=T.w[:]).then_inc(sem.lda, 16)
+    Y.dma_start(out=T.base[0:32, :], in_=T.nx[:]).then_inc(sem.lda, 16)
+    S.dma_start(out=T.ei[:, :], in_=T.e[:]).then_inc(sem.lde, 16)
+    Y.dma_start(out=T.xi[:, :], in_=T.x[:]).then_inc(sem.lde, 16)
+
+    v_z = fill(T.w0[:, 0:256], 0)
+    v_lr = fill(T.lrb[0:68, :, :, :], 0.0)
+    v_w0 = fill(T.w0[:, 256:ZC], 0)
+    S.wait_ge(sem.v, v_z)
+    for c in range(ZC, 2048, 256):
+        s_w0 = act(T.w0[:, c:c + 256], T.w0[:, 0:256])
+    Y.wait_ge(sem.v, v_w0)
+    Y.wait_ge(sem.s, s_w0)
+    Y.dma_start(out=T.w0[1:128:16, :], in_=T.nx[:]).then_inc(sem.lw, 16)
+    Y.dma_start(out=T.w0[8:128:16, :], in_=T.w[:]).then_inc(sem.lw, 16)
+    g_b = iota(T.base[64:68, :], [[1, 512]], 512)
+
+    V.wait_ge(sem.ldl, 16)
+    v_l = vcopy(T.l1[:, :], T.lst[:, :])
+    V.wait_ge(sem.lda, 32)
+    V.wait_ge(sem.gi, g_b)
+    v_b = vcopy(T.b16[0:68, 0:256], T.base[0:68, 0:256])
+    S.wait_ge(sem.lda, 32)
+    S.wait_ge(sem.gi, g_b)
+    s_b = act(T.b16[0:68, 256:512], T.base[0:68, 256:512])
+
+    fill(al("sh1"), 0.0)
+    n = fill(T.rr[:, :], 0.0)
+    vw(n)
+    v_rr = fill(T.rr[:, 15:144:16], 1.0)
+    v_s2 = fill(al("sh2"), 0.0)
+    V.wait_ge(sem.lde, 32)
+    v_eu = vcopy(T.eu[:, :], T.ei[:, :])
+    S.wait_ge(sem.v, v_rr)
+    for name in ("sh4", "zz"):
+        act(al(name), T.rr[:, 0:128], AF.Copy, 0.0, 0.0)
+    s_c = act(al("one"), T.rr[:, 0:128], AF.Copy, 1.0, 0.0)
+
+    g.wait_ge(sem.v, v_lr)
+    for rows, r0, r1, pattern in (((0, 32), 1, 2, [[-1, 4], [-4, 8], [0, 1]]),
+                                  ((64, 68), 0, 1, [[-1, 4], [0, 8], [0, 1]]),
+                                  ((32, 64), 8, 16, [[-1, 4], [-4, 8], [0, 8]])):
+        g.wait_ge(sem.gi, cnt["gi"])
+        ap = T.lrb[rows[0]:rows[1], :, :, r0:r1]
+        g_lr = sel(ap, ap, pattern, A.not_equal, 1.0, 0, 1)
+    g.wait_ge(sem.gi, g_lr)
+
+    def shifts(m):
+        sh = T["sh%d" % m]
+        k = 8 + 2 * m if m > 1 else 9
+        for r0, r1 in ((m + 1, min(2 * m + 1, 8)), (8 + m, k)):
+            if r1 > r0:
+                n = sel(sh[:, :, r0:r1], sh[:, :, r0:r1], [[-16, 8], [-1, r1 - r0]], A.not_equal, 1.0, m - r0, 1)
+        if k < 16:
+            n = sel(sh[:, :, k:16], sh[:, :, k:16], [[-16, 8], [0, 16 - k]], A.not_equal, 1.0, -7 - m, 1)
+        return n
+
+    g.wait_ge(sem.v, v_rr)
+    g_sh = {1: shifts(1)}
+    g.wait_ge(sem.v, v_s2)
+    g_sh[2] = shifts(2)
+    g.wait_ge(sem.s, s_c)
+    g_ht = iota(T.ht[:, :], [[2048, 2], [0, 8]])
+    sel(T.rep[0:16, :, :], T.zz[0:16, :, :], [[0, 8], [1, 16]], A.not_equal, 1.0, 0, -1)
+    n = sel(T.m16[0:16, :, :], T.zz[0:16, 0:2, 0:8], [[0, 2], [1, 8]], A.not_equal, 1.0, 0, -1)
+    g.wait_ge(sem.gi, n)
+    n = sel(T.m16[0:16, :, 1:8], T.m16[0:16, :, 1:8], [[0, 2], [1, 7]], A.not_equal, 1.0, 8, -1)
+    g.wait_ge(sem.gi, n)
+    g_m = sel(T.m16[0:16, 1:2, :], T.m16[0:16, 1:2, :], [[0, 1], [0, 8]], A.not_equal, 1.0, 15, -1)
+    g_sh[4] = shifts(4)
+    g_y = sel(T.y4[:, :], T.rr[:, :], [[-16, 9], [0, 16]], A.is_equal, 0.0, -4, 1)
+
+    def send(out, src, d, name):
+        dst = peer(d)
+        rid, pid = topo.addr(dst, core)
+        g.remote_dma(out, src, sem[name], sem.loc, pid, rid, topo.mask(core, dst))
+        cnt["loc"] += len(topo.engines(core, dst))
+
+    def landed(d):
+        return len(topo.engines(peer(-d), core))
+
+    g.wait_ge(sem.v, v_eu)
+    for t in (1, 2, 3):
+        send(T["le%d" % t][:, :], T.eu[:, 16 * t:min(16 * t + 32, 64)], t, "ad%d" % t)
+
+    tabs = {1: (T.w0, T.tb), 2: (T.tb, T.ta), 4: (T.ta, T.win)}
+    lists = {1: T.l1, 2: T.l2, 4: T.l4}
+    gs = {1: T.g1, 2: T.g2, 4: T.g3}
+    banks = {1: (0, 1, 2, 3), 2: (0, 1, 5, 7), 4: (0, 1, 2, 3)}
+    mine = {1: (0, 1), 2: (0, 1), 4: (0, 2, 1)}
+    v_ev, s_ev = v_w0, s_w0
+    for m in (1, 2, 4):
+        old, new = tabs[m]
+        G, L, sh, bank = gs[m], lists[m], al("sh%d" % m), [ps[b] for b in banks[m]]
+        ind = lambda q: old[:, 0:2048].indirect(L[:, 32 * q:32 * q + 32])
+        if m == 1:
+            V.wait_ge(sem.lw, 32)
+            S.wait_ge(sem.lw, 32)
+        vw(max(v_ev, v_l))
+        V.wait_ge(sem.s, s_ev)
+        S.wait_ge(sem.v, max(v_ev, v_l))
+        S.wait_ge(sem.s, s_ev)
+        got = {}
+        for q in (0, 2):
+            got[q] = vcopy(cols(G, q), ind(q))
+        for q in (1, 3):
+            got[q] = act(cols(G, q), ind(q))
+        if m < 4:
+            Y.wait_ge(sem.v, got[2])
+            Y.wait_ge(sem.s, got[3])
+            Y.dma_start(out=T["lf%d" % m][:, :], in_=G[m:128:16, :]).then_inc(sem["lx%d" % m], 16)
+
+        if m == 1:
+            PE.wait_ge(sem.v, v_b)
+            PE.wait_ge(sem.s, s_b)
+            PE.wait_ge(sem.gi, g_lr)
+        for q in (0, 2, 1, 3):
+            if m == 1 or q not in mine[m]:
+                mm(bank[q][:, :], T.lrb[0:68, q, :, :], T.b16[0:68, :], True, False, False)
+
+        def moves(m, q, f, lhsT, out, start, stop):
+            G = gs[m]
+            n = 0
+            if m == 1:
+                todo = [(out[:, 128 * (i % 4) + 64 * f:128 * (i % 4) + 64 * f + 64], G[:, 1024 * f + i:1024 * f + 1024:16])
+                        for i in range(4 * q, 4 * q + 4)]
+            elif m == 2:
+                todo = [(out[:, x:512:8], G[:, 256 * x + 64 * q:256 * x + 64 * q + 64]) for x in range(4 * f, 4 * f + 4)]
+            else:
+                todo = [(out[:, :], G[:, 1024 * f + q // 2:1024 * f + 1024:2])] if q % 2 == f else []
+            for i, (o, r) in enumerate(todo):
+                last = stop and i == len(todo) - 1
+                n = mm(o, lhsT, r, start and i == 0, last, last)
+            return n
+
+        for q in range(4):
+            if m > 1 and q not in mine[m]:
+                for k in (1, 2):
+                    if k < m:
+                        for f in (0, 1):
+                            moves(k, q, f, al("sh%d" % k), bank[q], False, False)
+        PE.wait_ge(sem.gi, g_sh[m])
+        pc = {}
+        for f in (0, 1):
+            PE.wait_ge(sem.v, got[2 * f])
+            PE.wait_ge(sem.s, got[2 * f + 1])
+            for q in (0, 2, 1, 3):
+                fresh = m > 1 and q in mine[m]
+                n = moves(m, q, f, sh, bank[q], fresh and (f == 0 or m == 4), f == 1 or m == 4)
+                if n:
+                    pc[q] = n
+        if m == 4:
+            s_nf = act(T.nfar[0:16, :], T.b16[0:16, 0:256], AF.Copy, -FAR, 0.0)
+            S.wait_ge(sem.gi, g_ht)
+            S.wait_ge(sem.v, v_eu)
+            s_hx = {0: act(T.hx0[:, :], T.ht[:, :].indirect(T.eu[:, 16:32])), 3: 0}
+        for q in mine[m]:
+            V.wait_ge(sem.pe, pc[q])
+            v_ev = tt(cols(new, q), cols(old, q), bank[q][:, :]) if m > 1 else vcopy(cols(new, q), bank[q][:, :])
+        for q in range(4):
+            if q not in mine[m]:
+                S.wait_ge(sem.pe, pc[q])
+                s_ev = act(cols(new, q), bank[q][:, :])
+        if m < 4:
+            V.wait_ge(sem["lx%d" % m], 16)
+            v_l = vcopy(lists[2 * m][:, :], T["lf%d" % m][:, :])
+        if m == 1:
+            PE.wait_ge(sem.gi, g_m)
+            p_mt = mm(ps[6][:, 0:16], T.rep[0:16, :, :], T.m16[0:16, :, :], True, True)
+
+    PE.wait_ge(sem.gi, g_y)
+    for h in (0, 1):
+        for b in range(16):
+            px = mm(ps[4][:, 64 * h:64 * h + 64], T.y4[:, 15 - b:143 - b], T.g3[:, 2 * b + h:2048:32], b == 0, b == 15, b == 15)
+
+    V.wait_ge(sem.pe, p_mt)
+    v_mt = vcopy(T.mt[:, :], ps[6][:, 0:16])
+    n = ts(T.hi0[:, :], T.ei[:, 0:16], A.is_ge, 8, A.mult, 2048.0)
+    vw(n)
+    n = tt(T.xo[:, :], T.xi[:, :], T.hi0[:, :])
+    vw(n)
+    vcopy(T.off0[:, :], T.xo[:, :])
+    S.wait_ge(sem.v, v_mt)
+    act(T.mk0[:, 0:128], T.mt[:, :].indirect(T.eu[:, 0:8]))
+    V.wait_ge(sem.pe, px)
+    v_l = vcopy(T.l8[:, :], ps[4][:, 0:128])
+
+    n = sel(al("s1"), al("one"), [[16, 8], [0, 16]], A.is_ge, 0.0, 7, -1)
+    n2 = iota(T.sd[:, :], [[0, 256]])
+    sel(al("idn"), al("zz"), [[-16, 8], [-1, 16]], A.not_equal, 1.0, 0, 1)
+    g.wait_ge(sem.gi, n)
+    sel(al("sums"), al("s1"), [[-16, 8], [0, 16]], A.is_ge, 0.0, 0, 1)
+    g.wait_ge(sem.gi, n2)
+    sel(T.sd[:, :], T.sd[:, :], [[0, 16], [1, 16]], A.not_equal, -BIG, 0, 0)
+    n = sel(al("w1"), al("one"), [[16, 8], [0, 16]], A.is_ge, 0.0, 15, -1)
+    g.wait_ge(sem.s, s_nf)
+    g_v = sel(T.far[0:16, :], T.nfar[0:16, :], [[0, 16], [1, 16]], A.not_equal, 0.0, 0, -1)
+    g.wait_ge(sem.gi, n)
+    sel(al("sumw"), al("w1"), [[-16, 8], [0, 16]], A.is_ge, 0.0, -8, 1)
+    g_w = sel(T.repf[0:16, :, :], T.zz[0:16, :, :], [[0, 8], [1, 16]], A.not_equal, 64.0, 0, -1)
+
+    win = T.win[:, 0:4096]
+    vw(max(v_ev, v_l))
+    V.wait_ge(sem.s, s_ev)
+    S.wait_ge(sem.v, v_l)
+    S.wait_ge(sem.s, s_ev)
+    n = vcopy(T.win[:, 2048:2048 + CUT], T.win[:, 0:2048].indirect(T.l8[:, 0:CUT // 16]))
+    s_w = act(T.win[:, 2048 + CUT:4096], T.win[:, 0:2048].indirect(T.l8[:, CUT // 16:128]))
+    vw(n)
+    V.wait_ge(sem.s, s_w)
+
+    s_mk = {0: act(T.mk0[:, 128:256], T.mt[:, :].indirect(T.eu[:, 8:16]))}
+    for t in (1, 2, 3):
+        S.wait_ge(sem["ad%d" % t], landed(t))
+        le = T["le%d" % t]
+        s_mk[t] = act(T["mk%d" % t][:, :], T.mt[:, :].indirect(le[:, 0:16]))
+        if t < 3:
+            s_hx[t] = act(T["hx%d" % t][:, :], T.ht[:, :].indirect(le[:, 16:32]))
+
+    half = lambda t, h: t[:, 128 * h:128 * h + 128]
+    part = lambda t, h: t[:, 8 * h:8 * h + 8]
+
+    def visit(t, v_free):
+        off = T["land%d" % t] if t else T.off0
+        M, mk, fin = T["mm%d" % t], T["mk%d" % t], t == 3
+        if t:
+            V.wait_ge(sem.s, s_mk[t])
+        if t == 1:
+            V.wait_ge(sem.cp, 16)
+        vg = []
+        for h in (0, 1):
+            if t:
+                V.wait_ge(sem["hop%d%d" % (t, h)], landed(1))
+            elif h:
+                V.wait_ge(sem.s, s_mk[0])
+            vg.append(tt(half(M, h), win.indirect(part(off, h)), half(mk, h), A.mult))
+        PE.wait_ge(sem.v, v_free)
+        PE.wait_ge(sem.gi, g_v if t == 0 else g_w)
+        PE.wait_ge(sem.s, s_hx[t])
+        for h in (0, 1):
+            mm(ps[6 + h][:, 0:128], (T.repf if fin else T.rep)[0:16, :, :], T.far[0:16, 0:128], True, False, False)
+            if not fin:
+                mm(ps[6 + h][:, 0:128], al("idn"), half(T["hx%d" % t], h), False, False, False)
+        pr = []
+        for h in (0, 1):
+            PE.wait_ge(sem.v, vg[h])
+            pr.append(mm(ps[6 + h][:, 0:128], al("sumf" if fin else "sums"), half(M, h), False, True))
+        out = T.fo if fin else T["ho%d" % t]
+        if t == 0:
+            V.wait_ge(sem.gi, g_v)
+        for h in (0, 1):
+            V.wait_ge(sem.pe, pr[h])
+            n = done("v", V.tensor_tensor_scan(out=half(T.sc, h), data0=T.sd[:, 0:128],
+                                               data1=ps[6 + h][:, 0:128], initial=0.0, op0=A.add, op1=A.max))
+            vw(n)
+            c = vcopy(part(out, h), T.sc[:, 128 * h + 15:128 * h + 128:16])
+            if not fin:
+                g.wait_ge(sem.v, c)
+                send(part(T["land%d" % (t + 1)], h), part(out, h), 1, "hop%d%d" % (t + 1, h))
+        return vg[1], c
+
+    def weights(t, M, n, v_free):
+        PE.wait_ge(sem.v, max(n, v_free))
+        mm(ps[4][:, 0:256], T.rep[0:16, :, :], T.far[0:16, :], True, False, False)
+        p = mm(ps[4][:, 0:256], al("sumw"), M[:, :], False, True)
+        V.wait_ge(sem.pe, p)
+        n = done("v", V.tensor_tensor_scan(out=T.sw[:, :], data0=T.sd[:, :], data1=ps[4][:, 0:256],
+                                           initial=0.0, op0=A.add, op1=A.max))
+        vw(n)
+        return n, vcopy(T["wl%d" % t][:, :], T.sw[:, 15:256:16])
+
+    def report(t, n):
+        g.wait_ge(sem.v, n)
+        send(T["wr%d" % t][:, :], T["wl%d" % t][:, :], -t, "bg%d" % t)
+
+    vg, c = visit(0, v_l)
+    Y.wait_ge(sem.v, vg)
+    Y.dma_start(out=T.win[15:128:16, 2048:4096], in_=T.win[15:128:16, 0:2048]).then_inc(sem.cp, 16)
+    S.wait_ge(sem.cp, 16)
+    s_gw = act(T.gw[:, :], win.indirect(T.off0[:, :]))
+    V.wait_ge(sem.gi, g_w)
+    n = ts(al("f512"), al("sums"), A.mult, 512.0)
+    vw(n)
+    v_sf = tt(al("sumf"), al("f512"), al("sumw"))
+
+    vg, c = visit(1, c)
+    v_w, n = weights(1, T.mm1, vg, 0)
+    report(1, n)
+
+    vg, c = visit(2, c)
+    v_w, n = weights(2, T.mm2, vg, v_w)
+    report(2, n)
+    V.wait_ge(sem.s, s_gw)
+    v_m = tt(T.mw0[:, :], T.gw[:, :], T.mk0[:, :], A.mult)
+
+    vg, c = visit(3, max(c, v_sf))
+    g.wait_ge(sem.v, c)
+    send(T.fin[:, :], T.fo[:, :], 1, "hop4")
+
+    v_w, n = weights(0, T.mw0, v_m, v_w)
+    V.wait_ge(sem.bg1, landed(-1))
+    V.wait_ge(sem.bg2, landed(-2))
+    n1 = tt(T.acc1[:, :], T.wr1[:, :], T.wr2[:, :])
+    vw(n1)
+    vw(tt(T.acc[:, :], T.acc1[:, :], T.wl0[:, :]))
+
+    V.wait_ge(sem.hop4, landed(1))
+    n1 = ts(T.ft[:, :], T.fin[:, :], A.bitwise_and, 511)
+    n2 = ts(T.fp[:, :], T.fin[:, :], A.arith_shift_right, 9)
+    vw(n1)
+    v_t = tt(T.ot[:, :], T.ft[:, :], T.acc[:, :])
+    S.wait_ge(sem.v, n2)
+    n = act(T.ol[:, :], T.fp[:, :])
+    S.wait_ge(sem.s, n)
+    S.dma_start(out=T.last[:], in_=T.ol[:, :]).then_inc(sem.outs, 16)
+    Y.wait_ge(sem.v, v_t)
+    Y.dma_start(out=T.total[:], in_=T.ot[:, :]).then_inc(sem.outs, 16)
+
+    for name in ("loc", "v", "s", "pe", "gi"):
+        g.wait_ge(sem[name], cnt[name])
+    for name, n in (("outs", 32), ("lw", 32), ("cp", 16), ("lx1", 16), ("lx2", 16), ("lda", 32), ("ldl", 16), ("lde", 32)):
+        g.wait_ge(sem[name], n)

@@ -1,30 +1,40 @@
 from concourse.mybir import AluOpType as A, ActivationFunctionType as AF
 
 NV = 4
-BIG = 16777216.0
-FAR = 32768.0
-CUT = 1088
-ZC = 1280
+ROOT = 128.0
+MARK = ROOT * ROOT
+Z0, ZV, ZG = 192, 1088, 1664
+B0, B1, B2 = 2048, 4096, 6144
+CUT = (30, 32)
+CUT8 = 104
 
 SCRATCH = {"ps%d" % b: ("psum", [128, 512], "float32") for b in range(8)}
-for _n in ("sh1", "sh2", "sh4", "idn", "rep", "repf", "zz", "one", "s1", "sums", "w1", "sumw", "f512", "sumf"):
+for _n in ("rep", "s1", "sums", "l7"):
     SCRATCH[_n] = ("sbuf", [128, 8, 16], "float16")
-SCRATCH["m16"] = ("sbuf", [128, 2, 8], "float16")
+for _n in ("f1", "sf"):
+    SCRATCH[_n] = ("sbuf", [128, 2, 8, 8], "float16")
+SCRATCH["rep8"] = ("sbuf", [128, 16, 8], "float16")
+SCRATCH["l15"] = ("sbuf", [128, 8, 8], "float16")
 SCRATCH["lrb"] = ("sbuf", [128, 4, 8, 16], "float16")
+SCRATCH["cz"] = ("sbuf", [128, 4, 8, 16], "float16")
+SCRATCH["g3"] = ("sbuf", [128, 2, 1024], "float16")
+SCRATCH["lst"] = ("sbuf", [128, 2, 4, 16], "int32")
+SCRATCH["ex"] = ("sbuf", [128, 4, 32], "float16")
+SCRATCH["le"] = ("sbuf", [128, 3, 32], "float16")
+SCRATCH["wl"] = ("sbuf", [128, 3, 32], "float32")
 for _dt, _bufs in (
-        ("int32", "base 512 lst 128 w0 2048 xi 16 ei 64 fo 16 fin 16 fp 16 ft 16"),
-        ("float16", "b16 512 g1 2048 g2 2048 g3 2048 lf1 128 lf2 128 mm0 256 mm1 256 mm2 256 mm3 256 mw0 256"
-                    " hx0 256 hx1 256 hx2 256 nfar 256 far 256 rr 144 y4 144"),
-        ("uint16", "l1 128 l2 128 l4 128 l8 128 eu 64 le1 32 le2 32 le3 16 off0 16 ho0 16 ho1 16 ho2 16"
+        ("int32", "base 512 lt 128 win 8192 xi 16 ei 64 idt 128 idm 128"),
+        ("float16", "b16 512 g1 2048 g2 2048 lf1 128 lf2 128 mm0 256 mm1 256 mm2 256 mm3 256"
+                    " gx0 256 gx1 256 gx2 256 gx3 256 ends 656 y3 144 m16 24 h0 64 h1 64 h9 64"),
+        ("uint16", "l1 128 l2 128 l4 128 l8 128 eu 16 leu 48 offa 16 offb 16 ho0 16 ho1 16 ho2 16"
                    " land1 16 land2 16 land3 16"),
-        ("float32", "mt 16 ht 16 hi0 16 xo 16 sd 256 ta 2048 tb 2048 win 4096"
-                    " mk0 256 mk1 256 mk2 256 mk3 256 sc 256 sw 256 gw 256"
-                    " wl0 16 wl1 16 wl2 16 wr1 16 wr2 16 acc1 16 acc 16 ol 16 ot 16")):
+        ("float32", "mt 16 xo 16 ta 2048 mk0 256 mk1 256 mk2 256 mk3 256 sc 256 sw 256"
+                    " wr1 32 wr2 32 wr3 32 fo 32 fin 32")):
     _w = _bufs.split()
     for _i in range(0, len(_w), 2):
         SCRATCH[_w[_i]] = ("sbuf", [128, int(_w[_i + 1])], _dt)
-SEMAPHORES = ["v", "s", "pe", "gi", "lda", "ldl", "lde", "lw", "lx1", "lx2", "cp", "outs", "loc",
-              "ad1", "ad2", "ad3", "hop10", "hop11", "hop20", "hop21", "hop30", "hop31", "hop4", "bg1", "bg2"]
+SEMAPHORES = ["v", "s", "pe", "gi", "lda", "ldl", "lde", "ldx", "lw", "lid", "lx10", "lx11", "lx20", "lx21", "cp", "outs", "loc",
+              "ad1", "ad2", "hop10", "hop11", "hop20", "hop21", "hop30", "hop31", "hop4", "bg1", "bg2", "bg3"]
 
 
 def rank_program(g, core, T, topo):
@@ -35,6 +45,7 @@ def rank_program(g, core, T, topo):
     sem = T.sem
     peer = lambda d: T.cores[(rank + d) % NV]
     cnt = {"v": 0, "s": 0, "pe": 0, "gi": 0, "loc": 0}
+    near_in, near_out = (peer(d) in topo.cores_of(core) for d in (-1, 1))
 
     def done(name, ins):
         ins.then_inc(sem[name], 1)
@@ -58,6 +69,9 @@ def rank_program(g, core, T, topo):
     def fill(ap, c):
         return done("v", V.memset(ap, c))
 
+    def scan(out, bank, ends):
+        return done("v", V.tensor_tensor_scan(out=out, data0=bank, data1=ends, initial=0.0, op0=A.max, op1=A.add))
+
     def act(out, in_, func=AF.Copy, bias=0.0, scale=1.0):
         return done("s", S.activation(out=out, in_=in_, func=func, bias=bias, scale=scale))
 
@@ -72,81 +86,110 @@ def rank_program(g, core, T, topo):
         return done("gi", g.affine_select(out, in_, pattern, op, c, base, cm))
 
     ps = [T["ps%d" % b] for b in range(8)]
-    cols = lambda t, q: t[:, 512 * q:512 * q + 512]
+    cols = lambda t, q, at=0: t[:, at + 512 * q:at + 512 * q + 512]
     al = lambda name: T[name][:, :, :]
+    half = lambda t, h, at=0: t[:, at + 128 * h:at + 128 * h + 128]
+    part = lambda t, h: t[:, 8 * h:8 * h + 8]
+    sh = {1: T.cz[:, 0, :, :], 2: T.cz[:, 1, :, :], 4: T.cz[:, 2, :, :]}
+    zz = T.cz[:, 3, :, :]
+    rep = T.rep[0:16, :, :]
 
-    Y.dma_start(out=T.lst[:, :], in_=T.nx[:]).then_inc(sem.ldl, 16)
+    for k in (0, 1):
+        Y.dma_start(out=T.lst[:, k, :, :], in_=T.nx[k:8:2, :]).then_inc(sem.ldl, 16)
+    S.dma_start(out=T.base[0:32, :], in_=T.nx[:]).then_inc(sem.lda, 16)
     S.dma_start(out=T.base[32:64, :], in_=T.w[:]).then_inc(sem.lda, 16)
-    Y.dma_start(out=T.base[0:32, :], in_=T.nx[:]).then_inc(sem.lda, 16)
-    S.dma_start(out=T.ei[:, :], in_=T.e[:]).then_inc(sem.lde, 16)
-    Y.dma_start(out=T.xi[:, :], in_=T.x[:]).then_inc(sem.lde, 16)
 
-    v_z = fill(T.w0[:, 0:256], 0)
-    v_lr = fill(T.lrb[0:68, :, :, :], 0.0)
-    v_w0 = fill(T.w0[:, 256:ZC], 0)
+    v_z = fill(T.win[:, B0:B0 + Z0], 0)
+    v_w0 = fill(T.win[:, B0 + Z0:B0 + ZV], 0)
     S.wait_ge(sem.v, v_z)
-    for c in range(ZC, 2048, 256):
-        s_w0 = act(T.w0[:, c:c + 256], T.w0[:, 0:256])
-    Y.wait_ge(sem.v, v_w0)
-    Y.wait_ge(sem.s, s_w0)
-    Y.dma_start(out=T.w0[1:128:16, :], in_=T.nx[:]).then_inc(sem.lw, 16)
-    Y.dma_start(out=T.w0[8:128:16, :], in_=T.w[:]).then_inc(sem.lw, 16)
-    g_b = iota(T.base[64:68, :], [[1, 512]], 512)
+    for c in range(B0 + ZV, B0 + ZG, Z0):
+        s_w0 = act(T.win[:, c:c + Z0], T.win[:, B0:B0 + Z0])
+    g_w0 = iota(T.win[:, B0 + ZG:B1], [[0, 2048 - ZG]])
+    for Q, lane, src in ((Y, 0, T.nx), (S, 8, T.w)):
+        Q.wait_ge(sem.v, v_w0)
+        Q.wait_ge(sem.s, s_w0)
+        Q.wait_ge(sem.gi, g_w0)
+        Q.dma_start(out=T.win[lane:128:16, B0:B1], in_=src[:]).then_inc(sem.lw, 16)
+    Y.dma_start(out=T.ei[:, :], in_=T.e[:]).then_inc(sem.lde, 16)
+    Y.dma_start(out=T.xi[:, :], in_=T.x[:]).then_inc(sem.ldx, 16)
 
-    V.wait_ge(sem.ldl, 16)
-    v_l = vcopy(T.l1[:, :], T.lst[:, :])
-    V.wait_ge(sem.lda, 32)
-    V.wait_ge(sem.gi, g_b)
-    v_b = vcopy(T.b16[0:68, 0:256], T.base[0:68, 0:256])
-    S.wait_ge(sem.lda, 32)
-    S.wait_ge(sem.gi, g_b)
-    s_b = act(T.b16[0:68, 256:512], T.base[0:68, 256:512])
-
-    fill(al("sh1"), 0.0)
-    n = fill(T.rr[:, :], 0.0)
+    v_lr = fill(T.lrb[0:64, :, :, :], 0.0)
+    v_cz = fill(T.cz[:, :, :, :], 0.0)
+    v_en = fill(T.ends[:, :], 0.0)
+    g_id = iota(T.idt[:, :], [[1, 128]], 128)
+    vw(v_en)
+    V.wait_ge(sem.ldl, 32)
+    for b in range(4):
+        n = done("v", V.transpose(out=T.lt[:, b:128:4], in_=T.lst[:, :, b, :]))
+    v_rr = fill(T.ends[:, 512 + 7:656:8], -MARK)
     vw(n)
-    v_rr = fill(T.rr[:, 15:144:16], 1.0)
-    v_s2 = fill(al("sh2"), 0.0)
-    V.wait_ge(sem.lde, 32)
-    v_eu = vcopy(T.eu[:, :], T.ei[:, :])
-    S.wait_ge(sem.v, v_rr)
-    for name in ("sh4", "zz"):
-        act(al(name), T.rr[:, 0:128], AF.Copy, 0.0, 0.0)
-    s_c = act(al("one"), T.rr[:, 0:128], AF.Copy, 1.0, 0.0)
+    v_l = vcopy(T.l1[:, :], T.lt[:, :])
+    S.wait_ge(sem.lda, 32)
+    s_b = act(T.b16[0:64, :], T.base[0:64, :])
+
+    def exponents():
+        S.wait_ge(sem.lde, 16)
+        n = act(T.h0[:, :], T.ei[:, :], AF.Sign)
+        act(T.ex[:, :, 0:16], T.ei[:, :])
+        S.wait_ge(sem.s, n)
+        return act(T.h1[:, :], T.h0[:, :], AF.Copy, -MARK, 2048.0)
+
+    got = {}
+
+    def between(m):
+        if m == 1:
+            V.wait_ge(sem.gi, g_id)
+            got["id"] = ts(T.idm[:, :], T.idt[:, :], A.bitwise_and, 2047)
+            V.wait_ge(sem.s, s_h)
+            vw(ts(T.h9[:, :], T.ei[:, :], A.is_ge, 9, A.mult, 2048.0))
+            return tt(T.ex[:, 0:3, 16:32], T.h1[:, 16:64], T.h9[:, 16:64])
+        if m == 2:
+            V.wait_ge(sem.ldx, 16)
+            tt(T.xo[:, :], T.xi[:, :], T.h9[:, 0:16])
+            vcopy(T.eu[:, :], T.ei[:, 0:16])
+            V.wait_ge(sem.pe, p_mt)
+            return vcopy(T.mt[:, :], ps[4][:, 0:16])
+        fill(T.wl[0:64, :, :], 0.0)
+        return vcopy(T.offa[:, :], T.xo[:, :])
+
+    def ends(k, block):
+        return sel(T.ends[:, 256 * k + 15:256 * k + 256:16], block, [[0, 16]], A.is_equal, 0.0, 0, 0)
 
     g.wait_ge(sem.v, v_lr)
-    for rows, r0, r1, pattern in (((0, 32), 1, 2, [[-1, 4], [-4, 8], [0, 1]]),
-                                  ((64, 68), 0, 1, [[-1, 4], [0, 8], [0, 1]]),
-                                  ((32, 64), 8, 16, [[-1, 4], [-4, 8], [0, 8]])):
-        g.wait_ge(sem.gi, cnt["gi"])
-        ap = T.lrb[rows[0]:rows[1], :, :, r0:r1]
-        g_lr = sel(ap, ap, pattern, A.not_equal, 1.0, 0, 1)
-    g.wait_ge(sem.gi, g_lr)
+    for row, r0, r1 in ((0, 0, 1), (32, 8, 16)):
+        ap = T.lrb[0:row + 32, :, :, r0:r1]
+        g_lr = sel(ap, ap, [[-1, 4], [-4, 8], [0, r1 - r0]], A.not_equal, 1.0, -row, 1)
 
-    def shifts(m):
-        sh = T["sh%d" % m]
-        k = 8 + 2 * m if m > 1 else 9
-        for r0, r1 in ((m + 1, min(2 * m + 1, 8)), (8 + m, k)):
+    def shifts(m, k):
+        top = 8 + 2 * m - 1
+        for r0, r1 in ((m, 2 * m), (8 + m, top)):
             if r1 > r0:
-                n = sel(sh[:, :, r0:r1], sh[:, :, r0:r1], [[-16, 8], [-1, r1 - r0]], A.not_equal, 1.0, m - r0, 1)
-        if k < 16:
-            n = sel(sh[:, :, k:16], sh[:, :, k:16], [[-16, 8], [0, 16 - k]], A.not_equal, 1.0, -7 - m, 1)
-        return n
+                ap = T.cz[:, k, :, r0:r1]
+                sel(ap, ap, [[-16, 8], [-1, r1 - r0]], A.not_equal, 1.0, m - r0, 1)
+        ap = T.cz[:, k, :, top:16]
+        return sel(ap, ap, [[-16, 8], [0, 16 - top]], A.not_equal, 1.0, -7 - m, 1)
 
+    g.wait_ge(sem.v, v_cz)
+    g_sh = {1: shifts(1, 0), 2: shifts(2, 1)}
+    sel(rep, T.cz[0:16, 3, :, :], [[0, 8], [1, 16]], A.not_equal, ROOT, 0, -1)
+    n = sel(T.m16[0:16, 1:17], T.cz[0:16, 3, 0, :], [[0, 2], [1, 8]], A.not_equal, 1 / ROOT, 0, -1)
+    sel(T.m16[0:16, 0:1], T.cz[0:16, 3, 0, 0:1], [[0, 1]], A.not_equal, 1 / ROOT, 7, -1)
+    g.wait_ge(sem.gi, n)
+    g_m = sel(T.m16[0:16, 1:17], T.m16[0:16, 1:17], [[0, 2], [1, 8]], A.not_equal, 1 / ROOT, 8, -1)
+    g_sh[4] = shifts(4, 2)
     g.wait_ge(sem.v, v_rr)
-    g_sh = {1: shifts(1)}
-    g.wait_ge(sem.v, v_s2)
-    g_sh[2] = shifts(2)
-    g.wait_ge(sem.s, s_c)
-    g_ht = iota(T.ht[:, :], [[2048, 2], [0, 8]])
-    sel(T.rep[0:16, :, :], T.zz[0:16, :, :], [[0, 8], [1, 16]], A.not_equal, 1.0, 0, -1)
-    n = sel(T.m16[0:16, :, :], T.zz[0:16, 0:2, 0:8], [[0, 2], [1, 8]], A.not_equal, 1.0, 0, -1)
+    g_y = sel(T.y3[:, :], T.ends[:, 512:656], [[-16, 9], [-256, 2], [0, 8]], A.is_equal, 0.0, 256 - 3, 1)
+    n = sel(al("s1"), zz, [[-16, 8], [0, 16]], A.is_gt, 1.0, -7, 1)
     g.wait_ge(sem.gi, n)
-    n = sel(T.m16[0:16, :, 1:8], T.m16[0:16, :, 1:8], [[0, 2], [1, 7]], A.not_equal, 1.0, 8, -1)
-    g.wait_ge(sem.gi, n)
-    g_m = sel(T.m16[0:16, 1:2, :], T.m16[0:16, 1:2, :], [[0, 1], [0, 8]], A.not_equal, 1.0, 15, -1)
-    g_sh[4] = shifts(4)
-    g_y = sel(T.y4[:, :], T.rr[:, :], [[-16, 9], [0, 16]], A.is_equal, 0.0, -4, 1)
+    sel(al("l7"), al("s1"), [[-16, 8], [0, 16]], A.is_ge, 0.0, -7, 1)
+    g_s = sel(al("sums"), al("s1"), [[-16, 8], [0, 16]], A.is_ge, 0.0, 0, 1)
+
+    def answers():
+        n = sel(T.f1[:, :, :, :], zz, [[-8, 2], [-16, 8], [0, 8]], A.is_gt, 1.0, -7, 1)
+        sel(T.rep8[0:8, :, :], T.cz[0:8, 3, :, :], [[0, 16], [1, 8]], A.not_equal, ROOT, 0, -1)
+        sel(al("l15"), T.cz[:, 3, 0:4, :], [[-16, 8], [0, 8]], A.not_equal, 1.0, -15, 1)
+        g.wait_ge(sem.gi, n)
+        return sel(T.sf[:, :, :, :], T.f1[:, :, :, :], [[-8, 2], [-16, 8], [0, 8]], A.is_ge, 0.0, 0, 1)
 
     def send(out, src, d, name):
         dst = peer(d)
@@ -157,244 +200,246 @@ def rank_program(g, core, T, topo):
     def landed(d):
         return len(topo.engines(peer(-d), core))
 
-    g.wait_ge(sem.v, v_eu)
-    for t in (1, 2, 3):
-        send(T["le%d" % t][:, :], T.eu[:, 16 * t:min(16 * t + 32, 64)], t, "ad%d" % t)
+    def marks(out, n):
+        for c in range(0, n, 128):
+            mm(out[:, c:c + 128], rep, rep, c == 0, False, False)
 
-    tabs = {1: (T.w0, T.tb), 2: (T.tb, T.ta), 4: (T.ta, T.win)}
+    tabs = {1: (T.win, B0, T.win, 0), 2: (T.win, 0, T.ta, 0), 4: (T.ta, 0, T.win, B1)}
     lists = {1: T.l1, 2: T.l2, 4: T.l4}
     gs = {1: T.g1, 2: T.g2, 4: T.g3}
-    banks = {1: (0, 1, 2, 3), 2: (0, 1, 5, 7), 4: (0, 1, 2, 3)}
-    mine = {1: (0, 1), 2: (0, 1), 4: (0, 2, 1)}
-    v_ev, s_ev = v_w0, s_w0
+    bank = {1: (0, 1, 2, 3), 2: (0, 6, 2, 7), 4: (0, 1, 2, 3)}
+
+    def first(q, out):
+        mm(out[:, :], T.lrb[0:64, q, :, :], T.b16[0:64, :], True, False, False)
+
+    def moves(m, q, out, start, stop):
+        G, o, b = gs[m], 1024 * (q // 2), q % 2
+        if m == 1:
+            todo = [(out[:, :], cols(G, q))]
+        elif m == 2:
+            todo = [(out[:, 64 * i:64 * i + 64], G[:, o + 8 * b + i:o + 1024:16]) for i in range(8)]
+        else:
+            todo = [(out[:, x:512:4], G[:, q // 2, 256 * x + 128 * b:256 * x + 128 * b + 128]) for x in range(4)]
+        for i, (a, r) in enumerate(todo):
+            last = stop and i == len(todo) - 1
+            n = mm(a, sh[m], r, start and i == 0, last, last)
+        return n
+
+    def relist(m, f):
+        V.wait_ge(sem["lx%d%d" % (m, f)], 16)
+        return vcopy(lists[2 * m][:, 64 * f:64 * f + 64], T["lf%d" % m][:, 64 * f:64 * f + 64])
+
+    V.wait_ge(sem.lw, 32)
+    S.wait_ge(sem.lw, 32)
+    PE.wait_ge(sem.s, s_b)
+    PE.wait_ge(sem.gi, g_lr)
+    for q in range(4):
+        first(q, ps[q])
+    s_ev = s_w0
     for m in (1, 2, 4):
-        old, new = tabs[m]
-        G, L, sh, bank = gs[m], lists[m], al("sh%d" % m), [ps[b] for b in banks[m]]
-        ind = lambda q: old[:, 0:2048].indirect(L[:, 32 * q:32 * q + 32])
-        if m == 1:
-            V.wait_ge(sem.lw, 32)
-            S.wait_ge(sem.lw, 32)
-        vw(max(v_ev, v_l))
+        old, o, new, at = tabs[m]
+        G, L = gs[m], lists[m]
+        ind = lambda a, b: old[:, o:o + 2048].indirect(L[:, a:b])
         V.wait_ge(sem.s, s_ev)
-        S.wait_ge(sem.v, max(v_ev, v_l))
         S.wait_ge(sem.s, s_ev)
-        got = {}
-        for q in (0, 2):
-            got[q] = vcopy(cols(G, q), ind(q))
-        for q in (1, 3):
-            got[q] = act(cols(G, q), ind(q))
-        if m < 4:
-            Y.wait_ge(sem.v, got[2])
-            Y.wait_ge(sem.s, got[3])
-            Y.dma_start(out=T["lf%d" % m][:, :], in_=G[m:128:16, :]).then_inc(sem["lx%d" % m], 16)
-
-        if m == 1:
-            PE.wait_ge(sem.v, v_b)
-            PE.wait_ge(sem.s, s_b)
-            PE.wait_ge(sem.gi, g_lr)
-        for q in (0, 2, 1, 3):
-            if m == 1 or q not in mine[m]:
-                mm(bank[q][:, :], T.lrb[0:68, q, :, :], T.b16[0:68, :], True, False, False)
-
-        def moves(m, q, f, lhsT, out, start, stop):
-            G = gs[m]
-            n = 0
-            if m == 1:
-                todo = [(out[:, 128 * (i % 4) + 64 * f:128 * (i % 4) + 64 * f + 64], G[:, 1024 * f + i:1024 * f + 1024:16])
-                        for i in range(4 * q, 4 * q + 4)]
-            elif m == 2:
-                todo = [(out[:, x:512:8], G[:, 256 * x + 64 * q:256 * x + 64 * q + 64]) for x in range(4 * f, 4 * f + 4)]
-            else:
-                todo = [(out[:, :], G[:, 1024 * f + q // 2:1024 * f + 1024:2])] if q % 2 == f else []
-            for i, (o, r) in enumerate(todo):
-                last = stop and i == len(todo) - 1
-                n = mm(o, lhsT, r, start and i == 0, last, last)
-            return n
-
-        for q in range(4):
-            if m > 1 and q not in mine[m]:
-                for k in (1, 2):
-                    if k < m:
-                        for f in (0, 1):
-                            moves(k, q, f, al("sh%d" % k), bank[q], False, False)
         PE.wait_ge(sem.gi, g_sh[m])
         pc = {}
         for f in (0, 1):
-            PE.wait_ge(sem.v, got[2 * f])
-            PE.wait_ge(sem.s, got[2 * f + 1])
-            for q in (0, 2, 1, 3):
-                fresh = m > 1 and q in mine[m]
-                n = moves(m, q, f, sh, bank[q], fresh and (f == 0 or m == 4), f == 1 or m == 4)
-                if n:
-                    pc[q] = n
-        if m == 4:
-            s_nf = act(T.nfar[0:16, :], T.b16[0:16, 0:256], AF.Copy, -FAR, 0.0)
-            S.wait_ge(sem.gi, g_ht)
-            S.wait_ge(sem.v, v_eu)
-            s_hx = {0: act(T.hx0[:, :], T.ht[:, :].indirect(T.eu[:, 16:32])), 3: 0}
-        for q in mine[m]:
-            V.wait_ge(sem.pe, pc[q])
-            v_ev = tt(cols(new, q), cols(old, q), bank[q][:, :]) if m > 1 else vcopy(cols(new, q), bank[q][:, :])
-        for q in range(4):
-            if q not in mine[m]:
-                S.wait_ge(sem.pe, pc[q])
-                s_ev = act(cols(new, q), bank[q][:, :])
+            if f and m > 1:
+                v_l = got[m] = relist(m // 2, 1)
+            vw(v_l)
+            S.wait_ge(sem.v, v_l)
+            a, b, c = 64 * f, 64 * f + CUT[f], 64 * f + 64
+            vg = vcopy(G[:, 16 * a:16 * b] if m < 4 else G[:, f, 0:16 * CUT[f]], ind(a, b))
+            sg = act(G[:, 16 * b:16 * c] if m < 4 else G[:, f, 16 * CUT[f]:1024], ind(b, c))
+            if m < 4:
+                Y.wait_ge(sem.v, vg)
+                Y.wait_ge(sem.s, sg)
+                Y.dma_start(out=T["lf%d" % m][:, a:c], in_=G[m - 1:128:16, 16 * a:16 * c]).then_inc(sem["lx%d%d" % (m, f)], 16)
+            PE.wait_ge(sem.v, vg)
+            PE.wait_ge(sem.s, sg)
+            for q in ((0, 1), (3, 2))[f]:
+                pc[q] = moves(m, q, ps[bank[m][q]], m > 1 and q % 2 == 0, True)
+            if m == 4 and f == 0:
+                for b in (6, 7):
+                    marks(ps[b], 128)
         if m < 4:
-            V.wait_ge(sem["lx%d" % m], 16)
-            v_l = vcopy(lists[2 * m][:, :], T["lf%d" % m][:, :])
+            for q in (1, 3):
+                first(q, ps[bank[2 * m][q]])
+                for k in (1, 2)[:m]:
+                    moves(k, q, ps[bank[2 * m][q]], False, False)
         if m == 1:
             PE.wait_ge(sem.gi, g_m)
-            p_mt = mm(ps[6][:, 0:16], T.rep[0:16, :, :], T.m16[0:16, :, :], True, True)
+            p_mt = mm(ps[4][:, 0:16], rep, T.m16[0:16, 0:16], True, True)
+            marks(ps[5], 256)
+            s_h = exponents()
+        for q in (0, 2):
+            V.wait_ge(sem.pe, pc[q])
+            v_l = tt(cols(new, q, at), cols(old, q), ps[q][:, :]) if m > 1 else vcopy(cols(new, q), ps[q][:, :])
+            if q == 0:
+                v_ex = between(m)
+                if m < 4:
+                    relist(m, 0)
+        for q in (1, 3):
+            S.wait_ge(sem.pe, pc[q])
+            s_ev = act(cols(new, q, at), ps[bank[m][q]][:, :])
+        if m == 1:
+            Y.wait_ge(sem.v, got["id"])
+            Y.dma_start(out=T.win[7:128:16, B0:B1], in_=T.idm[:, :]).then_inc(sem.lid, 16)
+            g.wait_ge(sem.v, v_ex)
+            ends(0, T.h1[:, 0:16])
+            g_e = {0: ends(1, T.ex[:, 0, 16:32]), 3: 0}
+        if m == 2:
+            S.wait_ge(sem.v, v_ex)
+            s_mk = {0: act(T.mk0[:, :], T.mt[:, :].indirect(T.eu[:, :]))}
+            Y.wait_ge(sem.v, v_l)
+            Y.dma_start(out=T.win[15:128:16, 0:B0], in_=T.win[15:128:16, B0:B1]).then_inc(sem.cp, 16)
+            g.wait_ge(sem.v, got[2])
+            for t in (1, 2, 3):
+                k = 32 if t < 3 else 16
+                send(T.le[:, t - 1, 0:k], T.ex[:, t, 0:k], t, "ad%d" % min(t, 2))
+            g_w = answers()
+    v_ev = v_l
 
     PE.wait_ge(sem.gi, g_y)
-    for h in (0, 1):
-        for b in range(16):
-            px = mm(ps[4][:, 64 * h:64 * h + 64], T.y4[:, 15 - b:143 - b], T.g3[:, 2 * b + h:2048:32], b == 0, b == 15, b == 15)
+    for i in range(16):
+        at = 256 * (i % 4)
+        p8 = mm(ps[4][:, 0:128], T.y3[:, 15 - i:143 - i], T.g3[:, :, at + i // 4:at + 256:4], i == 0, i == 15, i == 15)
 
-    V.wait_ge(sem.pe, p_mt)
-    v_mt = vcopy(T.mt[:, :], ps[6][:, 0:16])
-    n = ts(T.hi0[:, :], T.ei[:, 0:16], A.is_ge, 8, A.mult, 2048.0)
-    vw(n)
-    n = tt(T.xo[:, :], T.xi[:, :], T.hi0[:, :])
-    vw(n)
-    vcopy(T.off0[:, :], T.xo[:, :])
-    S.wait_ge(sem.v, v_mt)
-    act(T.mk0[:, 0:128], T.mt[:, :].indirect(T.eu[:, 0:8]))
-    V.wait_ge(sem.pe, px)
-    v_l = vcopy(T.l8[:, :], ps[4][:, 0:128])
+    def eight(copy, a, b):
+        return copy(T.win[:, B2 + 16 * a:B2 + 16 * b], T.win[:, B1:B2].indirect(T.l8[:, a:b]))
 
-    n = sel(al("s1"), al("one"), [[16, 8], [0, 16]], A.is_ge, 0.0, 7, -1)
-    n2 = iota(T.sd[:, :], [[0, 256]])
-    sel(al("idn"), al("zz"), [[-16, 8], [-1, 16]], A.not_equal, 1.0, 0, 1)
-    g.wait_ge(sem.gi, n)
-    sel(al("sums"), al("s1"), [[-16, 8], [0, 16]], A.is_ge, 0.0, 0, 1)
-    g.wait_ge(sem.gi, n2)
-    sel(T.sd[:, :], T.sd[:, :], [[0, 16], [1, 16]], A.not_equal, -BIG, 0, 0)
-    n = sel(al("w1"), al("one"), [[16, 8], [0, 16]], A.is_ge, 0.0, 15, -1)
-    g.wait_ge(sem.s, s_nf)
-    g_v = sel(T.far[0:16, :], T.nfar[0:16, :], [[0, 16], [1, 16]], A.not_equal, 0.0, 0, -1)
-    g.wait_ge(sem.gi, n)
-    sel(al("sumw"), al("w1"), [[-16, 8], [0, 16]], A.is_ge, 0.0, -8, 1)
-    g_w = sel(T.repf[0:16, :, :], T.zz[0:16, :, :], [[0, 8], [1, 16]], A.not_equal, 64.0, 0, -1)
+    def mask(t):
+        s_mk[t] = act(T["mk%d" % t][:, :], T.mt[:, :].indirect(T.leu[:, 16 * t - 16:16 * t]))
 
-    win = T.win[:, 0:4096]
-    vw(max(v_ev, v_l))
+    low, win, back = T.win[:, B0:B2], T.win[:, B0:B2 + 2048], T.win[:, 0:B2]
+    vw(v_ev)
     V.wait_ge(sem.s, s_ev)
-    S.wait_ge(sem.v, v_l)
+    V.wait_ge(sem.lid, 16)
+    S.wait_ge(sem.v, v_ev)
     S.wait_ge(sem.s, s_ev)
-    n = vcopy(T.win[:, 2048:2048 + CUT], T.win[:, 0:2048].indirect(T.l8[:, 0:CUT // 16]))
-    s_w = act(T.win[:, 2048 + CUT:4096], T.win[:, 0:2048].indirect(T.l8[:, CUT // 16:128]))
+    S.wait_ge(sem.lid, 16)
+    vg = vcopy(half(T.gx0, 0), low.indirect(part(T.offa, 0)))
+    s_x = {0: act(half(T.gx0, 1), low.indirect(part(T.offa, 1)))}
+    V.wait_ge(sem.ad1, landed(1))
+    S.wait_ge(sem.v, vcopy(T.leu[:, 0:16], T.le[:, 0, 0:16]))
+    mask(1)
+    PE.wait_ge(sem.gi, g_s)
+    PE.wait_ge(sem.v, vg)
+    PE.wait_ge(sem.s, s_x[0])
+    n = mm(ps[5][:, 0:256], al("l7"), T.gx0[:, :], False, True)
+    V.wait_ge(sem.pe, p8)
+    v8 = ts(T.l8[:, :], ps[4][:, 0:128], A.mult, -1 / MARK)
+    V.wait_ge(sem.pe, n)
+    V.wait_ge(sem.gi, g_e[0])
+    n = scan(T.sc[:, :], ps[5][:, 0:256], T.ends[:, 0:256])
     vw(n)
-    V.wait_ge(sem.s, s_w)
+    vw(vcopy(T.offb[:, :], T.sc[:, 15:256:16]))
+    S.wait_ge(sem.v, v8)
+    s_w = eight(act, 0, CUT8)
+    S.wait_ge(sem.cp, 16)
 
-    s_mk = {0: act(T.mk0[:, 128:256], T.mt[:, :].indirect(T.eu[:, 8:16]))}
-    for t in (1, 2, 3):
-        S.wait_ge(sem["ad%d" % t], landed(t))
-        le = T["le%d" % t]
-        s_mk[t] = act(T["mk%d" % t][:, :], T.mt[:, :].indirect(le[:, 0:16]))
-        if t < 3:
-            s_hx[t] = act(T["hx%d" % t][:, :], T.ht[:, :].indirect(le[:, 16:32]))
+    banks = {0: (6, 7), 1: (1, 2), 2: (3, 5), 3: (6, 7)}
 
-    half = lambda t, h: t[:, 128 * h:128 * h + 128]
-    part = lambda t, h: t[:, 8 * h:8 * h + 8]
-
-    def visit(t, v_free):
-        off = T["land%d" % t] if t else T.off0
+    def visit(t):
+        off = T["land%d" % t] if t else T.offb
         M, mk, fin = T["mm%d" % t], T["mk%d" % t], t == 3
-        if t:
-            V.wait_ge(sem.s, s_mk[t])
-        if t == 1:
-            V.wait_ge(sem.cp, 16)
-        vg = []
+        V.wait_ge(sem.s, s_mk[t])
+        vg, pr = [], []
         for h in (0, 1):
             if t:
-                V.wait_ge(sem["hop%d%d" % (t, h)], landed(1))
-            elif h:
-                V.wait_ge(sem.s, s_mk[0])
-            vg.append(tt(half(M, h), win.indirect(part(off, h)), half(mk, h), A.mult))
-        PE.wait_ge(sem.v, v_free)
-        PE.wait_ge(sem.gi, g_v if t == 0 else g_w)
-        PE.wait_ge(sem.s, s_hx[t])
-        for h in (0, 1):
-            mm(ps[6 + h][:, 0:128], (T.repf if fin else T.rep)[0:16, :, :], T.far[0:16, 0:128], True, False, False)
-            if not fin:
-                mm(ps[6 + h][:, 0:128], al("idn"), half(T["hx%d" % t], h), False, False, False)
-        pr = []
-        for h in (0, 1):
+                if near_in or h == 0:
+                    V.wait_ge(sem["hop%d%d" % (t, h)], landed(1))
+                    S.wait_ge(sem["hop%d%d" % (t, h)], landed(1))
+                s_x[t] = act(half(T["gx%d" % t], h), back.indirect(part(off, h)))
+            vg.append(tt(half(M, h), (win if t else low).indirect(part(off, h)), half(mk, h), A.mult))
+            out = ps[banks[t][h]]
+            if fin:
+                PE.wait_ge(sem.s, s_x[t])
+                mm(out[64:128, 0:128], al("l15"), half(T.gx3, h), False, False, False)
             PE.wait_ge(sem.v, vg[h])
-            pr.append(mm(ps[6 + h][:, 0:128], al("sumf" if fin else "sums"), half(M, h), False, True))
-        out = T.fo if fin else T["ho%d" % t]
-        if t == 0:
-            V.wait_ge(sem.gi, g_v)
+            pr.append(mm(out[:, 0:128], T.sf[:, :, :, :] if fin else al("sums"), half(M, h), False, True))
+        V.wait_ge(sem.gi, g_e[t])
         for h in (0, 1):
             V.wait_ge(sem.pe, pr[h])
-            n = done("v", V.tensor_tensor_scan(out=half(T.sc, h), data0=T.sd[:, 0:128],
-                                               data1=ps[6 + h][:, 0:128], initial=0.0, op0=A.add, op1=A.max))
-            vw(n)
-            c = vcopy(part(out, h), T.sc[:, 128 * h + 15:128 * h + 128:16])
-            if not fin:
-                g.wait_ge(sem.v, c)
-                send(part(T["land%d" % (t + 1)], h), part(out, h), 1, "hop%d%d" % (t + 1, h))
-        return vg[1], c
+            out = ps[banks[t][h]]
+            if fin:
+                for j in (0, 1):
+                    n = scan(T.sc[:, 128 * j + 64 * h:128 * j + 64 * h + 64], out[:, j:128:2], T.ends[:, 512:576])
+                continue
+            n = scan(half(T.sc, h), out[:, 0:128], half(T.ends, h, 256 * (1 - t % 2)))
+            if near_out or h:
+                a = 8 * h if near_out else 0
+                vw(n)
+                n = vcopy(T["ho%d" % t][:, a:8 * h + 8], T.sc[:, 16 * a + 15:128 * h + 128:16])
+                g.wait_ge(sem.v, n)
+                send(T["land%d" % (t + 1)][:, a:8 * h + 8], T["ho%d" % t][:, a:8 * h + 8], 1, "hop%d%d" % (t + 1, a // 8))
+        return n
 
-    def weights(t, M, n, v_free):
-        PE.wait_ge(sem.v, max(n, v_free))
-        mm(ps[4][:, 0:256], T.rep[0:16, :, :], T.far[0:16, :], True, False, False)
-        p = mm(ps[4][:, 0:256], al("sumw"), M[:, :], False, True)
+    def marks8(out, rows, n):
+        for j in (0, 1):
+            mm(out[128 - rows:128, j:n:2], T.rep8[0:8, 0:rows // 8, :], T.rep8[0:8, 0:n // 16, :], j == 0, False, False)
+
+    def weights_sum(t, v_free):
+        PE.wait_ge(sem.v, v_free)
+        marks8(ps[0], 64, 256)
+        mm(ps[0][64:128, 0:256], T.sf[:, 1, :, :], T["mm%d" % t][:, :], False, False, False)
+        PE.wait_ge(sem.s, s_x[t])
+        return mm(ps[0][64:128, 0:256], al("l15"), T["gx%d" % t][:, :], False, True)
+
+    def weights_on(t, p):
         V.wait_ge(sem.pe, p)
-        n = done("v", V.tensor_tensor_scan(out=T.sw[:, :], data0=T.sd[:, :], data1=ps[4][:, 0:256],
-                                           initial=0.0, op0=A.add, op1=A.max))
+        for j in (0, 1):
+            n = scan(T.sw[64:128, 128 * j:128 * j + 128], ps[0][64:128, j:256:2], T.ends[64:128, 512:640])
         vw(n)
-        return n, vcopy(T["wl%d" % t][:, :], T.sw[:, 15:256:16])
+        if t:
+            V.wait_ge(sem["bg%d" % t], landed(1))
+            c = tt(T.wl[64:128, t, :], T.sw[64:128, 7:256:8], T["wr%d" % t][64:128, :])
+        else:
+            c = vcopy(T.wl[64:128, 0, :], T.sw[64:128, 7:256:8])
+        g.wait_ge(sem.v, c)
+        send(T["wr%d" % (t + 1)][:, :], T.wl[:, t, :], 1, "bg%d" % (t + 1))
+        return n
 
-    def report(t, n):
-        g.wait_ge(sem.v, n)
-        send(T["wr%d" % t][:, :], T["wl%d" % t][:, :], -t, "bg%d" % t)
+    visit(0)
+    g.wait_ge(sem.ad1, landed(1))
+    g_e[1] = ends(0, T.le[:, 0, 16:32])
+    g.wait_ge(sem.ad2, landed(2) + landed(3))
+    g_e[2] = ends(1, T.le[:, 1, 16:32])
+    v_w = eight(vcopy, CUT8, 128)
+    PE.wait_ge(sem.gi, g_w)
+    p = weights_sum(0, v_w - 1)
+    for t in (1, 2):
+        for h in (0, 1):
+            marks(ps[banks[t][h]], 128)
+    for h in (0, 1):
+        marks8(ps[banks[3][h]], 128, 128)
+    v_free = weights_on(0, p)
+    vw(v_w)
+    V.wait_ge(sem.s, s_w)
 
-    vg, c = visit(0, v_l)
-    Y.wait_ge(sem.v, vg)
-    Y.dma_start(out=T.win[15:128:16, 2048:4096], in_=T.win[15:128:16, 0:2048]).then_inc(sem.cp, 16)
-    S.wait_ge(sem.cp, 16)
-    s_gw = act(T.gw[:, :], win.indirect(T.off0[:, :]))
-    V.wait_ge(sem.gi, g_w)
-    n = ts(al("f512"), al("sums"), A.mult, 512.0)
-    vw(n)
-    v_sf = tt(al("sumf"), al("f512"), al("sumw"))
+    visit(1)
+    V.wait_ge(sem.ad2, landed(2) + landed(3))
+    S.wait_ge(sem.v, vcopy(T.leu[:, 16:48], T.le[:, 1:3, 0:16]))
+    mask(2)
+    v_free = weights_on(1, weights_sum(1, v_free))
 
-    vg, c = visit(1, c)
-    v_w, n = weights(1, T.mm1, vg, 0)
-    report(1, n)
+    visit(2)
+    mask(3)
+    weights_on(2, weights_sum(2, v_free))
 
-    vg, c = visit(2, c)
-    v_w, n = weights(2, T.mm2, vg, v_w)
-    report(2, n)
-    V.wait_ge(sem.s, s_gw)
-    v_m = tt(T.mw0[:, :], T.gw[:, :], T.mk0[:, :], A.mult)
-
-    vg, c = visit(3, max(c, v_sf))
+    vw(visit(3))
+    V.wait_ge(sem.bg3, landed(1))
+    c = tt(T.fo[:, :], T.sc[:, 7:256:8], T.wr3[:, :])
     g.wait_ge(sem.v, c)
     send(T.fin[:, :], T.fo[:, :], 1, "hop4")
 
-    v_w, n = weights(0, T.mw0, v_m, v_w)
-    V.wait_ge(sem.bg1, landed(-1))
-    V.wait_ge(sem.bg2, landed(-2))
-    n1 = tt(T.acc1[:, :], T.wr1[:, :], T.wr2[:, :])
-    vw(n1)
-    vw(tt(T.acc[:, :], T.acc1[:, :], T.wl0[:, :]))
-
-    V.wait_ge(sem.hop4, landed(1))
-    n1 = ts(T.ft[:, :], T.fin[:, :], A.bitwise_and, 511)
-    n2 = ts(T.fp[:, :], T.fin[:, :], A.arith_shift_right, 9)
-    vw(n1)
-    v_t = tt(T.ot[:, :], T.ft[:, :], T.acc[:, :])
-    S.wait_ge(sem.v, n2)
-    n = act(T.ol[:, :], T.fp[:, :])
-    S.wait_ge(sem.s, n)
-    S.dma_start(out=T.last[:], in_=T.ol[:, :]).then_inc(sem.outs, 16)
-    Y.wait_ge(sem.v, v_t)
-    Y.dma_start(out=T.total[:], in_=T.ot[:, :]).then_inc(sem.outs, 16)
+    for Q, out, c in ((S, T.last, 0), (Y, T.total, 64)):
+        Q.wait_ge(sem.hop4, landed(1))
+        Q.dma_start(out=out[:], in_=T.fin[c:c + 64, :]).then_inc(sem.outs, 16)
 
     for name in ("loc", "v", "s", "pe", "gi"):
         g.wait_ge(sem[name], cnt[name])
-    for name, n in (("outs", 32), ("lw", 32), ("cp", 16), ("lx1", 16), ("lx2", 16), ("lda", 32), ("ldl", 16), ("lde", 32)):
+    for name, n in (("outs", 32), ("lw", 32), ("cp", 16), ("lid", 16), ("lx10", 16), ("lx11", 16), ("lx20", 16), ("lx21", 16),
+                    ("lda", 32), ("ldl", 32), ("lde", 16), ("ldx", 16)):
         g.wait_ge(sem[name], n)

from concourse.mybir import AluOpType as A, ActivationFunctionType as AF

NV = 4
ROOT = 128.0
MARK = ROOT * ROOT
Z0, ZV, ZG = 192, 1088, 1664
B0, B1, B2 = 2048, 4096, 6144
CUT = (30, 32)
CUT8 = 104

SCRATCH = {"ps%d" % b: ("psum", [128, 512], "float32") for b in range(8)}
for _n in ("rep", "s1", "sums", "l7"):
    SCRATCH[_n] = ("sbuf", [128, 8, 16], "float16")
for _n in ("f1", "sf"):
    SCRATCH[_n] = ("sbuf", [128, 2, 8, 8], "float16")
SCRATCH["rep8"] = ("sbuf", [128, 16, 8], "float16")
SCRATCH["l15"] = ("sbuf", [128, 8, 8], "float16")
SCRATCH["lrb"] = ("sbuf", [128, 4, 8, 16], "float16")
SCRATCH["cz"] = ("sbuf", [128, 4, 8, 16], "float16")
SCRATCH["g3"] = ("sbuf", [128, 2, 1024], "float16")
SCRATCH["lst"] = ("sbuf", [128, 2, 4, 16], "int32")
SCRATCH["ex"] = ("sbuf", [128, 4, 32], "float16")
SCRATCH["le"] = ("sbuf", [128, 3, 32], "float16")
SCRATCH["wl"] = ("sbuf", [128, 3, 32], "float32")
for _dt, _bufs in (
        ("int32", "base 512 lt 128 win 8192 xi 16 ei 64 idt 128 idm 128"),
        ("float16", "b16 512 g1 2048 g2 2048 lf1 128 lf2 128 mm0 256 mm1 256 mm2 256 mm3 256"
                    " gx0 256 gx1 256 gx2 256 gx3 256 ends 656 y3 144 m16 24 h0 64 h1 64 h9 64"),
        ("uint16", "l1 128 l2 128 l4 128 l8 128 eu 16 leu 48 offa 16 offb 16 ho0 16 ho1 16 ho2 16"
                   " land1 16 land2 16 land3 16"),
        ("float32", "mt 16 xo 16 ta 2048 mk0 256 mk1 256 mk2 256 mk3 256 sc 256 sw 256"
                    " wr1 32 wr2 32 wr3 32 fo 32 fin 32")):
    _w = _bufs.split()
    for _i in range(0, len(_w), 2):
        SCRATCH[_w[_i]] = ("sbuf", [128, int(_w[_i + 1])], _dt)
SEMAPHORES = ["v", "s", "pe", "gi", "lda", "ldl", "lde", "ldx", "lw", "lid", "lx10", "lx11", "lx20", "lx21", "cp", "outs", "loc",
              "ad1", "ad2", "hop10", "hop11", "hop20", "hop21", "hop30", "hop31", "hop4", "bg1", "bg2", "bg3"]


def rank_program(g, core, T, topo):
    rank = T.rank_of(core)
    if rank is None:
        return
    V, S, PE, Y = g.vector, g.scalar, g.tensor, g.sync
    sem = T.sem
    peer = lambda d: T.cores[(rank + d) % NV]
    cnt = {"v": 0, "s": 0, "pe": 0, "gi": 0, "loc": 0}
    near_in, near_out = (peer(d) in topo.cores_of(core) for d in (-1, 1))

    def done(name, ins):
        ins.then_inc(sem[name], 1)
        cnt[name] += 1
        return cnt[name]

    def vw(n):
        V.wait_ge(sem.v, n)

    def ts(out, in0, op, c, op1=None, c1=None):
        if op1 is None:
            return done("v", V.tensor_scalar(out=out, in0=in0, scalar1=c, scalar2=None, op0=op))
        return done("v", V.tensor_scalar(out=out, in0=in0, scalar1=c, scalar2=c1, op0=op, op1=op1))

    def tt(out, in0, in1, op=A.add):
        return done("v", V.tensor_tensor(out=out, in0=in0, in1=in1, op=op))

    def vcopy(out, in_):
        return done("v", V.tensor_copy(out=out, in_=in_))

    def fill(ap, c):
        return done("v", V.memset(ap, c))

    def scan(out, bank, ends):
        return done("v", V.tensor_tensor_scan(out=out, data0=bank, data1=ends, initial=0.0, op0=A.max, op1=A.add))

    def act(out, in_, func=AF.Copy, bias=0.0, scale=1.0):
        return done("s", S.activation(out=out, in_=in_, func=func, bias=bias, scale=scale))

    def mm(out, lhsT, rhs, start, stop, count=True):
        ins = PE.matmul(out=out, lhsT=lhsT, rhs=rhs, start=start, stop=stop)
        return done("pe", ins) if count else 0

    def iota(ap, pattern, cm=0, base=0):
        return done("gi", g.iota(ap, pattern, base, cm, allow_small_or_imprecise_dtypes=True))

    def sel(out, in_, pattern, op, c, base, cm):
        return done("gi", g.affine_select(out, in_, pattern, op, c, base, cm))

    ps = [T["ps%d" % b] for b in range(8)]
    cols = lambda t, q, at=0: t[:, at + 512 * q:at + 512 * q + 512]
    al = lambda name: T[name][:, :, :]
    half = lambda t, h, at=0: t[:, at + 128 * h:at + 128 * h + 128]
    part = lambda t, h: t[:, 8 * h:8 * h + 8]
    sh = {1: T.cz[:, 0, :, :], 2: T.cz[:, 1, :, :], 4: T.cz[:, 2, :, :]}
    zz = T.cz[:, 3, :, :]
    rep = T.rep[0:16, :, :]

    for k in (0, 1):
        Y.dma_start(out=T.lst[:, k, :, :], in_=T.nx[k:8:2, :]).then_inc(sem.ldl, 16)
    S.dma_start(out=T.base[0:32, :], in_=T.nx[:]).then_inc(sem.lda, 16)
    S.dma_start(out=T.base[32:64, :], in_=T.w[:]).then_inc(sem.lda, 16)

    v_z = fill(T.win[:, B0:B0 + Z0], 0)
    v_w0 = fill(T.win[:, B0 + Z0:B0 + ZV], 0)
    S.wait_ge(sem.v, v_z)
    for c in range(B0 + ZV, B0 + ZG, Z0):
        s_w0 = act(T.win[:, c:c + Z0], T.win[:, B0:B0 + Z0])
    g_w0 = iota(T.win[:, B0 + ZG:B1], [[0, 2048 - ZG]])
    for Q, lane, src in ((Y, 0, T.nx), (S, 8, T.w)):
        Q.wait_ge(sem.v, v_w0)
        Q.wait_ge(sem.s, s_w0)
        Q.wait_ge(sem.gi, g_w0)
        Q.dma_start(out=T.win[lane:128:16, B0:B1], in_=src[:]).then_inc(sem.lw, 16)
    Y.dma_start(out=T.ei[:, :], in_=T.e[:]).then_inc(sem.lde, 16)
    Y.dma_start(out=T.xi[:, :], in_=T.x[:]).then_inc(sem.ldx, 16)

    v_lr = fill(T.lrb[0:64, :, :, :], 0.0)
    v_cz = fill(T.cz[:, :, :, :], 0.0)
    v_en = fill(T.ends[:, :], 0.0)
    g_id = iota(T.idt[:, :], [[1, 128]], 128)
    vw(v_en)
    V.wait_ge(sem.ldl, 32)
    for b in range(4):
        n = done("v", V.transpose(out=T.lt[:, b:128:4], in_=T.lst[:, :, b, :]))
    v_rr = fill(T.ends[:, 512 + 7:656:8], -MARK)
    vw(n)
    v_l = vcopy(T.l1[:, :], T.lt[:, :])
    S.wait_ge(sem.lda, 32)
    s_b = act(T.b16[0:64, :], T.base[0:64, :])

    def exponents():
        S.wait_ge(sem.lde, 16)
        n = act(T.h0[:, :], T.ei[:, :], AF.Sign)
        act(T.ex[:, :, 0:16], T.ei[:, :])
        S.wait_ge(sem.s, n)
        return act(T.h1[:, :], T.h0[:, :], AF.Copy, -MARK, 2048.0)

    got = {}

    def between(m):
        if m == 1:
            V.wait_ge(sem.gi, g_id)
            got["id"] = ts(T.idm[:, :], T.idt[:, :], A.bitwise_and, 2047)
            V.wait_ge(sem.s, s_h)
            vw(ts(T.h9[:, :], T.ei[:, :], A.is_ge, 9, A.mult, 2048.0))
            return tt(T.ex[:, 0:3, 16:32], T.h1[:, 16:64], T.h9[:, 16:64])
        if m == 2:
            V.wait_ge(sem.ldx, 16)
            tt(T.xo[:, :], T.xi[:, :], T.h9[:, 0:16])
            vcopy(T.eu[:, :], T.ei[:, 0:16])
            V.wait_ge(sem.pe, p_mt)
            return vcopy(T.mt[:, :], ps[4][:, 0:16])
        fill(T.wl[0:64, :, :], 0.0)
        return vcopy(T.offa[:, :], T.xo[:, :])

    def ends(k, block):
        return sel(T.ends[:, 256 * k + 15:256 * k + 256:16], block, [[0, 16]], A.is_equal, 0.0, 0, 0)

    g.wait_ge(sem.v, v_lr)
    for row, r0, r1 in ((0, 0, 1), (32, 8, 16)):
        ap = T.lrb[0:row + 32, :, :, r0:r1]
        g_lr = sel(ap, ap, [[-1, 4], [-4, 8], [0, r1 - r0]], A.not_equal, 1.0, -row, 1)

    def shifts(m, k):
        top = 8 + 2 * m - 1
        for r0, r1 in ((m, 2 * m), (8 + m, top)):
            if r1 > r0:
                ap = T.cz[:, k, :, r0:r1]
                sel(ap, ap, [[-16, 8], [-1, r1 - r0]], A.not_equal, 1.0, m - r0, 1)
        ap = T.cz[:, k, :, top:16]
        return sel(ap, ap, [[-16, 8], [0, 16 - top]], A.not_equal, 1.0, -7 - m, 1)

    g.wait_ge(sem.v, v_cz)
    g_sh = {1: shifts(1, 0), 2: shifts(2, 1)}
    sel(rep, T.cz[0:16, 3, :, :], [[0, 8], [1, 16]], A.not_equal, ROOT, 0, -1)
    n = sel(T.m16[0:16, 1:17], T.cz[0:16, 3, 0, :], [[0, 2], [1, 8]], A.not_equal, 1 / ROOT, 0, -1)
    sel(T.m16[0:16, 0:1], T.cz[0:16, 3, 0, 0:1], [[0, 1]], A.not_equal, 1 / ROOT, 7, -1)
    g.wait_ge(sem.gi, n)
    g_m = sel(T.m16[0:16, 1:17], T.m16[0:16, 1:17], [[0, 2], [1, 8]], A.not_equal, 1 / ROOT, 8, -1)
    g_sh[4] = shifts(4, 2)
    g.wait_ge(sem.v, v_rr)
    g_y = sel(T.y3[:, :], T.ends[:, 512:656], [[-16, 9], [-256, 2], [0, 8]], A.is_equal, 0.0, 256 - 3, 1)
    n = sel(al("s1"), zz, [[-16, 8], [0, 16]], A.is_gt, 1.0, -7, 1)
    g.wait_ge(sem.gi, n)
    sel(al("l7"), al("s1"), [[-16, 8], [0, 16]], A.is_ge, 0.0, -7, 1)
    g_s = sel(al("sums"), al("s1"), [[-16, 8], [0, 16]], A.is_ge, 0.0, 0, 1)

    def answers():
        n = sel(T.f1[:, :, :, :], zz, [[-8, 2], [-16, 8], [0, 8]], A.is_gt, 1.0, -7, 1)
        sel(T.rep8[0:8, :, :], T.cz[0:8, 3, :, :], [[0, 16], [1, 8]], A.not_equal, ROOT, 0, -1)
        sel(al("l15"), T.cz[:, 3, 0:4, :], [[-16, 8], [0, 8]], A.not_equal, 1.0, -15, 1)
        g.wait_ge(sem.gi, n)
        return sel(T.sf[:, :, :, :], T.f1[:, :, :, :], [[-8, 2], [-16, 8], [0, 8]], A.is_ge, 0.0, 0, 1)

    def send(out, src, d, name):
        dst = peer(d)
        rid, pid = topo.addr(dst, core)
        g.remote_dma(out, src, sem[name], sem.loc, pid, rid, topo.mask(core, dst))
        cnt["loc"] += len(topo.engines(core, dst))

    def landed(d):
        return len(topo.engines(peer(-d), core))

    def marks(out, n):
        for c in range(0, n, 128):
            mm(out[:, c:c + 128], rep, rep, c == 0, False, False)

    tabs = {1: (T.win, B0, T.win, 0), 2: (T.win, 0, T.ta, 0), 4: (T.ta, 0, T.win, B1)}
    lists = {1: T.l1, 2: T.l2, 4: T.l4}
    gs = {1: T.g1, 2: T.g2, 4: T.g3}
    bank = {1: (0, 1, 2, 3), 2: (0, 6, 2, 7), 4: (0, 1, 2, 3)}

    def first(q, out):
        mm(out[:, :], T.lrb[0:64, q, :, :], T.b16[0:64, :], True, False, False)

    def moves(m, q, out, start, stop):
        G, o, b = gs[m], 1024 * (q // 2), q % 2
        if m == 1:
            todo = [(out[:, :], cols(G, q))]
        elif m == 2:
            todo = [(out[:, 64 * i:64 * i + 64], G[:, o + 8 * b + i:o + 1024:16]) for i in range(8)]
        else:
            todo = [(out[:, x:512:4], G[:, q // 2, 256 * x + 128 * b:256 * x + 128 * b + 128]) for x in range(4)]
        for i, (a, r) in enumerate(todo):
            last = stop and i == len(todo) - 1
            n = mm(a, sh[m], r, start and i == 0, last, last)
        return n

    def relist(m, f):
        V.wait_ge(sem["lx%d%d" % (m, f)], 16)
        return vcopy(lists[2 * m][:, 64 * f:64 * f + 64], T["lf%d" % m][:, 64 * f:64 * f + 64])

    V.wait_ge(sem.lw, 32)
    S.wait_ge(sem.lw, 32)
    PE.wait_ge(sem.s, s_b)
    PE.wait_ge(sem.gi, g_lr)
    for q in range(4):
        first(q, ps[q])
    s_ev = s_w0
    for m in (1, 2, 4):
        old, o, new, at = tabs[m]
        G, L = gs[m], lists[m]
        ind = lambda a, b: old[:, o:o + 2048].indirect(L[:, a:b])
        V.wait_ge(sem.s, s_ev)
        S.wait_ge(sem.s, s_ev)
        PE.wait_ge(sem.gi, g_sh[m])
        pc = {}
        for f in (0, 1):
            if f and m > 1:
                v_l = got[m] = relist(m // 2, 1)
            vw(v_l)
            S.wait_ge(sem.v, v_l)
            a, b, c = 64 * f, 64 * f + CUT[f], 64 * f + 64
            vg = vcopy(G[:, 16 * a:16 * b] if m < 4 else G[:, f, 0:16 * CUT[f]], ind(a, b))
            sg = act(G[:, 16 * b:16 * c] if m < 4 else G[:, f, 16 * CUT[f]:1024], ind(b, c))
            if m < 4:
                Y.wait_ge(sem.v, vg)
                Y.wait_ge(sem.s, sg)
                Y.dma_start(out=T["lf%d" % m][:, a:c], in_=G[m - 1:128:16, 16 * a:16 * c]).then_inc(sem["lx%d%d" % (m, f)], 16)
            PE.wait_ge(sem.v, vg)
            PE.wait_ge(sem.s, sg)
            for q in ((0, 1), (3, 2))[f]:
                pc[q] = moves(m, q, ps[bank[m][q]], m > 1 and q % 2 == 0, True)
            if m == 4 and f == 0:
                for b in (6, 7):
                    marks(ps[b], 128)
        if m < 4:
            for q in (1, 3):
                first(q, ps[bank[2 * m][q]])
                for k in (1, 2)[:m]:
                    moves(k, q, ps[bank[2 * m][q]], False, False)
        if m == 1:
            PE.wait_ge(sem.gi, g_m)
            p_mt = mm(ps[4][:, 0:16], rep, T.m16[0:16, 0:16], True, True)
            marks(ps[5], 256)
            s_h = exponents()
        for q in (0, 2):
            V.wait_ge(sem.pe, pc[q])
            v_l = tt(cols(new, q, at), cols(old, q), ps[q][:, :]) if m > 1 else vcopy(cols(new, q), ps[q][:, :])
            if q == 0:
                v_ex = between(m)
                if m < 4:
                    relist(m, 0)
        for q in (1, 3):
            S.wait_ge(sem.pe, pc[q])
            s_ev = act(cols(new, q, at), ps[bank[m][q]][:, :])
        if m == 1:
            Y.wait_ge(sem.v, got["id"])
            Y.dma_start(out=T.win[7:128:16, B0:B1], in_=T.idm[:, :]).then_inc(sem.lid, 16)
            g.wait_ge(sem.v, v_ex)
            ends(0, T.h1[:, 0:16])
            g_e = {0: ends(1, T.ex[:, 0, 16:32]), 3: 0}
        if m == 2:
            S.wait_ge(sem.v, v_ex)
            s_mk = {0: act(T.mk0[:, :], T.mt[:, :].indirect(T.eu[:, :]))}
            Y.wait_ge(sem.v, v_l)
            Y.dma_start(out=T.win[15:128:16, 0:B0], in_=T.win[15:128:16, B0:B1]).then_inc(sem.cp, 16)
            g.wait_ge(sem.v, got[2])
            for t in (1, 2, 3):
                k = 32 if t < 3 else 16
                send(T.le[:, t - 1, 0:k], T.ex[:, t, 0:k], t, "ad%d" % min(t, 2))
            g_w = answers()
    v_ev = v_l

    PE.wait_ge(sem.gi, g_y)
    for i in range(16):
        at = 256 * (i % 4)
        p8 = mm(ps[4][:, 0:128], T.y3[:, 15 - i:143 - i], T.g3[:, :, at + i // 4:at + 256:4], i == 0, i == 15, i == 15)

    def eight(copy, a, b):
        return copy(T.win[:, B2 + 16 * a:B2 + 16 * b], T.win[:, B1:B2].indirect(T.l8[:, a:b]))

    def mask(t):
        s_mk[t] = act(T["mk%d" % t][:, :], T.mt[:, :].indirect(T.leu[:, 16 * t - 16:16 * t]))

    low, win, back = T.win[:, B0:B2], T.win[:, B0:B2 + 2048], T.win[:, 0:B2]
    vw(v_ev)
    V.wait_ge(sem.s, s_ev)
    V.wait_ge(sem.lid, 16)
    S.wait_ge(sem.v, v_ev)
    S.wait_ge(sem.s, s_ev)
    S.wait_ge(sem.lid, 16)
    vg = vcopy(half(T.gx0, 0), low.indirect(part(T.offa, 0)))
    s_x = {0: act(half(T.gx0, 1), low.indirect(part(T.offa, 1)))}
    V.wait_ge(sem.ad1, landed(1))
    S.wait_ge(sem.v, vcopy(T.leu[:, 0:16], T.le[:, 0, 0:16]))
    mask(1)
    PE.wait_ge(sem.gi, g_s)
    PE.wait_ge(sem.v, vg)
    PE.wait_ge(sem.s, s_x[0])
    n = mm(ps[5][:, 0:256], al("l7"), T.gx0[:, :], False, True)
    V.wait_ge(sem.pe, p8)
    v8 = ts(T.l8[:, :], ps[4][:, 0:128], A.mult, -1 / MARK)
    V.wait_ge(sem.pe, n)
    V.wait_ge(sem.gi, g_e[0])
    n = scan(T.sc[:, :], ps[5][:, 0:256], T.ends[:, 0:256])
    vw(n)
    vw(vcopy(T.offb[:, :], T.sc[:, 15:256:16]))
    S.wait_ge(sem.v, v8)
    s_w = eight(act, 0, CUT8)
    S.wait_ge(sem.cp, 16)

    banks = {0: (6, 7), 1: (1, 2), 2: (3, 5), 3: (6, 7)}

    def visit(t):
        off = T["land%d" % t] if t else T.offb
        M, mk, fin = T["mm%d" % t], T["mk%d" % t], t == 3
        V.wait_ge(sem.s, s_mk[t])
        vg, pr = [], []
        for h in (0, 1):
            if t:
                if near_in or h == 0:
                    V.wait_ge(sem["hop%d%d" % (t, h)], landed(1))
                    S.wait_ge(sem["hop%d%d" % (t, h)], landed(1))
                s_x[t] = act(half(T["gx%d" % t], h), back.indirect(part(off, h)))
            vg.append(tt(half(M, h), (win if t else low).indirect(part(off, h)), half(mk, h), A.mult))
            out = ps[banks[t][h]]
            if fin:
                PE.wait_ge(sem.s, s_x[t])
                mm(out[64:128, 0:128], al("l15"), half(T.gx3, h), False, False, False)
            PE.wait_ge(sem.v, vg[h])
            pr.append(mm(out[:, 0:128], T.sf[:, :, :, :] if fin else al("sums"), half(M, h), False, True))
        V.wait_ge(sem.gi, g_e[t])
        for h in (0, 1):
            V.wait_ge(sem.pe, pr[h])
            out = ps[banks[t][h]]
            if fin:
                for j in (0, 1):
                    n = scan(T.sc[:, 128 * j + 64 * h:128 * j + 64 * h + 64], out[:, j:128:2], T.ends[:, 512:576])
                continue
            n = scan(half(T.sc, h), out[:, 0:128], half(T.ends, h, 256 * (1 - t % 2)))
            if near_out or h:
                a = 8 * h if near_out else 0
                vw(n)
                n = vcopy(T["ho%d" % t][:, a:8 * h + 8], T.sc[:, 16 * a + 15:128 * h + 128:16])
                g.wait_ge(sem.v, n)
                send(T["land%d" % (t + 1)][:, a:8 * h + 8], T["ho%d" % t][:, a:8 * h + 8], 1, "hop%d%d" % (t + 1, a // 8))
        return n

    def marks8(out, rows, n):
        for j in (0, 1):
            mm(out[128 - rows:128, j:n:2], T.rep8[0:8, 0:rows // 8, :], T.rep8[0:8, 0:n // 16, :], j == 0, False, False)

    def weights_sum(t, v_free):
        PE.wait_ge(sem.v, v_free)
        marks8(ps[0], 64, 256)
        mm(ps[0][64:128, 0:256], T.sf[:, 1, :, :], T["mm%d" % t][:, :], False, False, False)
        PE.wait_ge(sem.s, s_x[t])
        return mm(ps[0][64:128, 0:256], al("l15"), T["gx%d" % t][:, :], False, True)

    def weights_on(t, p):
        V.wait_ge(sem.pe, p)
        for j in (0, 1):
            n = scan(T.sw[64:128, 128 * j:128 * j + 128], ps[0][64:128, j:256:2], T.ends[64:128, 512:640])
        vw(n)
        if t:
            V.wait_ge(sem["bg%d" % t], landed(1))
            c = tt(T.wl[64:128, t, :], T.sw[64:128, 7:256:8], T["wr%d" % t][64:128, :])
        else:
            c = vcopy(T.wl[64:128, 0, :], T.sw[64:128, 7:256:8])
        g.wait_ge(sem.v, c)
        send(T["wr%d" % (t + 1)][:, :], T.wl[:, t, :], 1, "bg%d" % (t + 1))
        return n

    visit(0)
    g.wait_ge(sem.ad1, landed(1))
    g_e[1] = ends(0, T.le[:, 0, 16:32])
    g.wait_ge(sem.ad2, landed(2) + landed(3))
    g_e[2] = ends(1, T.le[:, 1, 16:32])
    v_w = eight(vcopy, CUT8, 128)
    PE.wait_ge(sem.gi, g_w)
    p = weights_sum(0, v_w - 1)
    for t in (1, 2):
        for h in (0, 1):
            marks(ps[banks[t][h]], 128)
    for h in (0, 1):
        marks8(ps[banks[3][h]], 128, 128)
    v_free = weights_on(0, p)
    vw(v_w)
    V.wait_ge(sem.s, s_w)

    visit(1)
    V.wait_ge(sem.ad2, landed(2) + landed(3))
    S.wait_ge(sem.v, vcopy(T.leu[:, 16:48], T.le[:, 1:3, 0:16]))
    mask(2)
    v_free = weights_on(1, weights_sum(1, v_free))

    visit(2)
    mask(3)
    weights_on(2, weights_sum(2, v_free))

    vw(visit(3))
    V.wait_ge(sem.bg3, landed(1))
    c = tt(T.fo[:, :], T.sc[:, 7:256:8], T.wr3[:, :])
    g.wait_ge(sem.v, c)
    send(T.fin[:, :], T.fo[:, :], 1, "hop4")

    for Q, out, c in ((S, T.last, 0), (Y, T.total, 64)):
        Q.wait_ge(sem.hop4, landed(1))
        Q.dma_start(out=out[:], in_=T.fin[c:c + 64, :]).then_inc(sem.outs, 16)

    for name in ("loc", "v", "s", "pe", "gi"):
        g.wait_ge(sem[name], cnt[name])
    for name, n in (("outs", 32), ("lw", 32), ("cp", 16), ("lid", 16), ("lx10", 16), ("lx11", 16), ("lx20", 16), ("lx21", 16),
                    ("lda", 32), ("ldl", 32), ("lde", 16), ("ldx", 16)):
        g.wait_ge(sem[name], n)
